import numpy as np
import ml_dtypes


def mxq(x, axis, fmt="e4m3"):
    dtype, down = {"e4m3": (ml_dtypes.float8_e4m3fn, 7), "e5m2": (ml_dtypes.float8_e5m2, 14)}[fmt]
    v = np.moveaxis(np.asarray(x, np.float32).astype(ml_dtypes.bfloat16).astype(np.float64), axis, -1)
    blocks = v.reshape(v.shape[:-1] + (-1, 32))
    amax = np.abs(blocks).max(-1, keepdims=True)
    byte = np.maximum(np.where(amax > 0, np.frexp(amax)[1] - 1 + 127, 0) - down, 1)
    scale = np.exp2(byte - 127.0)
    codes = (blocks / scale).astype(np.float32).astype(dtype).astype(np.float64)
    return np.moveaxis((codes * scale).reshape(v.shape), -1, axis)


WIDE = False


def mx_kscale(k):
    if not WIDE:
        return np.ones(k)
    levels = np.array([10, -10, 5, -5, 0])
    if k % 512:
        return np.exp2(np.random.permutation(np.resize(levels, k // 32))).repeat(32)
    a = np.empty((k // 512, 16))
    for p in range(k // 512):
        a[p, :8] = np.random.permutation(np.resize(levels, 8))
        for g in range(8):
            far = levels[np.abs(levels - a[p, g]) >= 10]
            a[p, g + 8] = far[np.random.randint(len(far))]
    return np.exp2(a.ravel()).repeat(32)


def f64(x):
    return np.asarray(x).astype(np.float64)


def striped(idx):
    return np.tile(idx.reshape(-1, 16).T, (8, 1)).astype(np.uint16)


def unstriped(offs):
    return offs[:16].T.reshape(-1).astype(np.int64)


E2M1 = np.array([0.0, 0.5, 1.0, 1.5, 2.0, 3.0, 4.0, 6.0, -0.0, -0.5, -1.0, -1.5, -2.0, -3.0, -4.0, -6.0])


def pack_fp4(w):
    k, n = w.shape
    w = f64(np.asarray(w, np.float32).astype(ml_dtypes.bfloat16)).reshape(k // 32, 32, n)
    amax = np.abs(w).max(1)
    mant, ex = np.frexp(amax / 6.0)
    byte = np.clip(np.where(amax > 0, np.where(mant > 0.5, ex, ex - 1) + 127, 1), 1, 254)
    scaled = (w * np.exp2(127.0 - byte)[:, None, :]).reshape(k, n).astype(np.float32)
    c = np.ascontiguousarray(scaled.reshape(k // 512, 128, 4, n).transpose(0, 1, 3, 2)).astype(ml_dtypes.float4_e2m1fn).view(np.uint8) & 0xF
    words = (c[..., 0::2] | (c[..., 1::2] << 4)).reshape(k // 512, 128, 2 * n)
    return np.ascontiguousarray(words), np.ascontiguousarray(byte.astype(np.uint8).reshape(k // 512, 16, n))


def unpack_fp4(words, scales):
    g, _, n = scales.shape
    words = np.ascontiguousarray(words).reshape(g, 128, n, 2)
    nib = np.empty((g, 128, n, 4), np.uint8)
    nib[..., 0::2] = words & 0xF
    nib[..., 1::2] = words >> 4
    vals = E2M1[nib] * np.repeat(np.exp2(scales.astype(np.float64) - 127.0), 8, axis=1)[..., None]
    return vals.transpose(0, 1, 3, 2).reshape(g * 512, n)


K, T, N = 1024, 1024, 128
P = 2 ** 7


def setup_inputs():
    n = np.random.standard_normal
    s = mx_kscale(K)[:, None]
    packed_xT = pack_fp4(n((K, T)) * s)
    return {
        "x_words": packed_xT[0],
        "x_scales": packed_xT[1],
        "w1": (n((K, N)) / np.sqrt(K) / s).astype(np.float32),
        "fx": np.tile(np.random.uniform(0.05, 0.95, T), (P, 1)).astype(np.float32),
        "fy": np.tile(np.random.uniform(0.05, 0.95, T), (P, 1)).astype(np.float32),
        "c00": striped(np.random.permutation(T)),
        "c01": striped(np.random.permutation(T)),
        "c10": striped(np.random.permutation(T)),
        "c11": striped(np.random.permutation(T)),
    }


def reference(x_words, x_scales, w1, fx, fy, c00, c01, c10, c11):
    xq = unpack_fp4(x_words, x_scales)
    y = mxq(f64(w1), 0, "e4m3").T @ xq
    top = y[:, unstriped(c00)] + (y[:, unstriped(c01)] - y[:, unstriped(c00)]) * f64(fx)[:1]
    low = y[:, unstriped(c10)] + (y[:, unstriped(c11)] - y[:, unstriped(c10)]) * f64(fx)[:1]
    return top + (low - top) * f64(fy)[:1]

@@ -1,0 +1,201 @@
+from contextlib import ExitStack
+
+import concourse.mybir as mybir
+from concourse.masks import make_identity
+
+K, T, M = 1024, 1024, 128
+FLOPS = 2 * K * T * M
+BYTES = K * T // 2 + K * T // 32 + 4 * K * M + 2 * 4 * T + 4 * 2 * T + 4 * M * T
+
+F32 = mybir.dt.float32
+BF16 = mybir.dt.bfloat16
+I32 = mybir.dt.int32
+U32 = mybir.dt.uint32
+U16 = mybir.dt.uint16
+U8 = mybir.dt.uint8
+FP8X4 = mybir.dt.float8_e4m3fn_x4
+FP4X4 = mybir.dt.float4_e2m1fn_x4
+MULT = mybir.AluOpType.mult
+COPY = mybir.ActivationFunctionType.Copy
+
+P = 128
+PASSES = 2
+BANK = 512
+CHUNKS = (256, 256, 256, 128)
+LAST = T - P
+ADD = mybir.AluOpType.add
+
+
+def tile_picked_wbilin_none_l_kernel(tc, x_words, x_scales, w1, fx, fy, c00, c01, c10, c11, out):
+    nc = tc.nc
+    with ExitStack() as ctx:
+        keep = ctx.enter_context(tc.tile_pool(name="keep", bufs=1))
+        psum = ctx.enter_context(tc.psum_pool(name="psum", bufs=1))
+
+        def bank(b):
+            return psum.tile([P, BANK], F32, name="bank%d" % b, tag="bank%d" % b)
+
+        x_planes = keep.tile([P, PASSES * T], U8, align_bytes=64)
+        nc.vector.memset(x_planes[:].bitcast(I32), 0)
+
+        w_raw = [keep.tile([P, 4, M], F32, name="w_raw%d" % z, tag="stage%d" % z) for z in range(PASSES)]
+        x_codes = [keep.tile([P, 2 * T], U8, name="x_codes%d" % z, align_bytes=64) for z in range(PASSES)]
+
+        def load_w(z):
+            nc.sync.dma_start(out=w_raw[z][:], in_=w1[512 * z : 512 * (z + 1), :].rearrange("(p j) m -> p j m", j=4))
+
+        def load_x(z):
+            nc.sync.dma_start(out=x_codes[z][:], in_=x_words[z])
+
+        load_w(0)
+        for q in range(4):
+            nc.sync.dma_start(
+                out=x_planes[32 * q : 32 * q + 4, :].bitcast(I32).rearrange("r (z c) -> r z c", z=PASSES),
+                in_=x_scales[:, 4 * q : 4 * q + 4, :].bitcast(I32).rearrange("z r c -> r z c"),
+            )
+        load_x(0)
+        load_w(1)
+        load_x(1)
+        first = CHUNKS[0]
+        fx_first = keep.tile([P, first], F32)
+        nc.sync.dma_start(out=fx_first[:], in_=fx[:, 0:first])
+        lists = {}
+        for name, src in (("c01", c01), ("c00", c00), ("c11", c11), ("c10", c10)):
+            lists[name] = keep.tile([P, T // 16], U16, name=name + "_offsets")
+            nc.sync.dma_start(lists[name][:], src)
+        fy_rows = keep.tile([P, P], F32)
+        nc.sync.dma_start(out=fy_rows[:], in_=fy[0:16, :].rearrange("r (b i) -> (r b) i", i=P))
+
+        ident = keep.tile([P, P], F32)
+        make_identity(nc, ident[:])
+
+        w_codes, w_planes = [], []
+        for z in range(PASSES):
+            grouped = keep.tile([P, M, 4], BF16, name="w_grouped%d" % z, align_bytes=64)
+            for h in range(2):
+                cols = slice(64 * h, 64 * (h + 1))
+                nc.vector.tensor_copy(out=grouped[:, cols, :], in_=w_raw[z][:, :, cols].rearrange("p j m -> p m j"))
+            codes = keep.tile([P, M], U32, name="w_codes%d" % z, align_bytes=64)
+            plane = keep.tile([P, M], U8, name="w_plane%d" % z, align_bytes=64)
+            for h in range(2):
+                cols = slice(64 * h, 64 * (h + 1))
+                nc.vector.quantize_mx(
+                    out=codes[:, cols].bitcast(FP8X4), scales=plane[:, cols], in_=grouped[:, cols, :].rearrange("p m j -> p (m j)")
+                )
+            w_codes.append(codes)
+            w_planes.append(plane)
+
+        fx_rest = keep.tile([P, T - first], F32, tag="stage1")
+        nc.sync.dma_start(out=fx_rest[:], in_=fx[:, first:T])
+
+        groups = [(0, 512)] + [(512 + 128 * i, 128) for i in range(4)]
+        sums = [bank(g) for g in range(len(groups))]
+        y = keep.tile([P, T], F32)
+        for z in range(PASSES):
+            for g, (c0, n) in enumerate(groups):
+                nc.tensor.matmul_mx(
+                    out=sums[g][:, 0:n],
+                    lhsT=w_codes[z][:].bitcast(FP8X4),
+                    lhsT_scale=w_planes[z][:],
+                    rhs=x_codes[z][:, 2 * c0 : 2 * (c0 + n)].bitcast(FP4X4),
+                    rhs_scale=x_planes[:, z * T + c0 : z * T + c0 + n],
+                    start=(z == 0),
+                    stop=(z == PASSES - 1),
+                )
+        for g, (c0, n) in enumerate(groups):
+            if g == 0:
+                nc.scalar.copy(out=y[:, c0 : c0 + n], in_=sums[g][:, 0:n])
+            else:
+                nc.vector.tensor_copy(out=y[:, c0 : c0 + n], in_=sums[g][:, 0:n])
+
+        gx_first = keep.tile([P, first], F32)
+        nc.scalar.activation(out=gx_first[:], in_=fx_first[:], func=COPY, scale=-1.0, bias=1.0)
+        gx_rest = keep.tile([P, LAST - first], F32)
+        nc.scalar.activation(out=gx_rest[:], in_=fx_rest[:, 0 : LAST - first], func=COPY, scale=-1.0, bias=1.0)
+
+        fy_bank = bank(0)
+        nc.tensor.transpose(fy_bank[:, 0:P], fy_rows[:], ident[:])
+        fy_col = keep.tile([P, 8], F32)
+        gy_col = keep.tile([P, 8], F32)
+        nc.scalar.copy(out=fy_col[:], in_=fy_bank[:, 0:8])
+        nc.scalar.activation(out=gy_col[:], in_=fy_bank[:, 0:8], func=COPY, scale=-1.0, bias=1.0)
+
+        def add_transposed(dst, terms):
+            for i, term in enumerate(terms):
+                nc.tensor.matmul(dst, lhsT=term, rhs=ident[:], start=(i == 0), stop=(i == len(terms) - 1), is_transpose=True)
+
+        def blk(b):
+            return slice(P * b, P * (b + 1))
+
+        fx_bank = bank(6)
+        nc.tensor.transpose(fx_bank[:, 0:P], fx_rest[:, LAST - first : T - first], ident[:])
+        gx_col = keep.tile([P, 1], F32)
+        nc.scalar.activation(out=gx_col[:], in_=fx_bank[:, 0:1], func=COPY, scale=-1.0, bias=1.0)
+        corner_col = keep.tile([P, 4], F32)
+        for i, (src, col) in enumerate(((fx_bank, gy_col), (fx_bank, fy_col), (gx_col, gy_col), (gx_col, fy_col))):
+            nc.scalar.activation(out=corner_col[:, i : i + 1], in_=src[:, 0:1], func=COPY, scale=col[:, 7:8])
+        corner_bank = bank(7)
+        for i in range(4):
+            nc.tensor.transpose(corner_bank[:, blk(i)], corner_col[:, i : i + 1].to_broadcast([P, P]), ident[:])
+        corner = keep.tile([P, 4 * P], F32)
+        nc.scalar.copy(out=corner[:], in_=corner_bank[:])
+
+        v0 = 0
+        use = 1
+        tail = keep.tile([P, 2 * P], F32)
+        for ci, n in enumerate(CHUNKS):
+            nb = n // P
+            scaled = []
+            for row, (right, left, col) in enumerate((("c01", "c00", gy_col), ("c11", "c10", fy_col))):
+                terms = []
+                if ci == 0:
+                    factors = (fx_first[:], gx_first[:])
+                else:
+                    factors = (fx_rest[:, v0 - first : v0 - first + n], gx_rest[:, v0 - first : v0 - first + n])
+                for name, factor in zip((right, left), factors):
+                    prod = keep.tile([P, n], F32, name="prod_%s_%d" % (name, ci))
+                    nc.vector.tensor_tensor(
+                        prod[:], y[:].indirect(lists[name][:, v0 // 16 : (v0 + n) // 16]), factor, MULT
+                    )
+                    terms.append(prod)
+                turned = bank(use % 8)
+                use = use + 1
+                for b in range(nb):
+                    add_transposed(turned[:, blk(b)], [t[:, blk(b)] for t in terms])
+                weighted = keep.tile([P, n], F32, name="weighted_%d_%d" % (row, ci))
+                for b in range(nb):
+                    vb = v0 // P + b
+                    nc.scalar.activation(out=weighted[:, blk(b)], in_=turned[:, blk(b)], func=COPY, scale=col[:, vb : vb + 1])
+                scaled.append(weighted)
+            back = bank(use % 8)
+            use = use + 1
+            for b in range(nb):
+                add_transposed(back[:, blk(b)], [t[:, blk(b)] for t in scaled])
+            if ci == len(CHUNKS) - 1:
+                nc.scalar.copy(out=tail[:, 0:P], in_=back[:, 0:n])
+            else:
+                result = keep.tile([P, n], F32, name="result_%d" % ci)
+                nc.scalar.copy(out=result[:], in_=back[:, 0:n])
+                nc.sync.dma_start(out=out[:, v0 : v0 + n], in_=result[:])
+            v0 = v0 + n
+
+        def last_product(name, i, a, b):
+            prod = keep.tile([P, b - a], F32, name="last_%s_%d" % (name, a))
+            nc.vector.tensor_tensor(
+                prod[:], y[:].indirect(lists[name][:, (LAST + a) // 16 : (LAST + b) // 16]), corner[:, P * i + a : P * i + b], MULT
+            )
+            return prod
+
+        half = P // 2
+        p01 = last_product("c01", 0, 0, P)
+        p00 = last_product("c00", 2, 0, P)
+        p11 = last_product("c11", 1, 0, P)
+        two = keep.tile([P, P], F32)
+        nc.vector.tensor_tensor(two[:], p01[:], p00[:], ADD)
+        p10a = last_product("c10", 3, 0, half)
+        three = keep.tile([P, P], F32)
+        nc.vector.tensor_tensor(three[:], two[:], p11[:], ADD)
+        p10b = last_product("c10", 3, half, P)
+        nc.vector.tensor_tensor(tail[:, P : P + half], three[:, 0:half], p10a[:], ADD)
+        nc.vector.tensor_tensor(tail[:, P + half : 2 * P], three[:, half:P], p10b[:], ADD)
+        nc.sync.dma_start(out=out[:, LAST - P : T], in_=tail[:])

@@ -38,24 +38,26 @@ def tile_picked_wbilin_none_l_kernel(tc, x_words, x_scales, w1, fx, fy, c00, c01
         x_planes = keep.tile([P, PASSES * T], U8, align_bytes=64)
         nc.vector.memset(x_planes[:].bitcast(I32), 0)
 
-        w_raw = [keep.tile([P, 4, M], F32, name="w_raw%d" % z, tag="stage%d" % z) for z in range(PASSES)]
-        x_codes = [keep.tile([P, 2 * T], U8, name="x_codes%d" % z, align_bytes=64) for z in range(PASSES)]
+        w_raw = [keep.tile([P, 4, M], F32, name="w_raw%d" % z) for z in range(PASSES)]
+        x_codes = [[keep.tile([P, 2 * BANK], U8, name="x_codes%d_%d" % (z, h), tag="x%d%d" % (z, h), align_bytes=64) for h in range(2)] for z in range(PASSES)]
 
         def load_w(z):
             nc.sync.dma_start(out=w_raw[z][:], in_=w1[512 * z : 512 * (z + 1), :].rearrange("(p j) m -> p j m", j=4))
 
-        def load_x(z):
-            nc.sync.dma_start(out=x_codes[z][:], in_=x_words[z])
+        def load_x(z, h):
+            nc.sync.dma_start(out=x_codes[z][h][:], in_=x_words[z][:, 2 * BANK * h : 2 * BANK * (h + 1)])
 
         load_w(0)
-        for q in range(4):
+        load_x(0, 0)
+        for r in range(4):
             nc.sync.dma_start(
-                out=x_planes[32 * q : 32 * q + 4, :].bitcast(I32).rearrange("r (z c) -> r z c", z=PASSES),
-                in_=x_scales[:, 4 * q : 4 * q + 4, :].bitcast(I32).rearrange("z r c -> r z c"),
+                out=x_planes[r:P:32, :].bitcast(I32).rearrange("q (z c) -> q z c", z=PASSES),
+                in_=x_scales[:, r:16:4, :].bitcast(I32).rearrange("z q c -> q z c"),
             )
-        load_x(0)
         load_w(1)
-        load_x(1)
+        load_x(0, 1)
+        load_x(1, 0)
+        load_x(1, 1)
         first = CHUNKS[0]
         fx_first = keep.tile([P, first], F32)
         nc.sync.dma_start(out=fx_first[:], in_=fx[:, 0:first])
@@ -85,7 +87,7 @@ def tile_picked_wbilin_none_l_kernel(tc, x_words, x_scales, w1, fx, fy, c00, c01
             w_codes.append(codes)
             w_planes.append(plane)
 
-        fx_rest = keep.tile([P, T - first], F32, tag="stage1")
+        fx_rest = keep.tile([P, T - first], F32)
         nc.sync.dma_start(out=fx_rest[:], in_=fx[:, first:T])
 
         groups = [(0, 512)] + [(512 + 128 * i, 128) for i in range(4)]
@@ -97,21 +99,20 @@ def tile_picked_wbilin_none_l_kernel(tc, x_words, x_scales, w1, fx, fy, c00, c01
                     out=sums[g][:, 0:n],
                     lhsT=w_codes[z][:].bitcast(FP8X4),
                     lhsT_scale=w_planes[z][:],
-                    rhs=x_codes[z][:, 2 * c0 : 2 * (c0 + n)].bitcast(FP4X4),
+                    rhs=x_codes[z][c0 // BANK][:, 2 * (c0 % BANK) : 2 * (c0 % BANK + n)].bitcast(FP4X4),
                     rhs_scale=x_planes[:, z * T + c0 : z * T + c0 + n],
                     start=(z == 0),
                     stop=(z == PASSES - 1),
                 )
         for g, (c0, n) in enumerate(groups):
             if g == 0:
-                nc.scalar.copy(out=y[:, c0 : c0 + n], in_=sums[g][:, 0:n])
-            else:
                 nc.vector.tensor_copy(out=y[:, c0 : c0 + n], in_=sums[g][:, 0:n])
+            else:
+                nc.scalar.copy(out=y[:, c0 : c0 + n], in_=sums[g][:, 0:n])
 
-        gx_first = keep.tile([P, first], F32)
-        nc.scalar.activation(out=gx_first[:], in_=fx_first[:], func=COPY, scale=-1.0, bias=1.0)
-        gx_rest = keep.tile([P, LAST - first], F32)
-        nc.scalar.activation(out=gx_rest[:], in_=fx_rest[:, 0 : LAST - first], func=COPY, scale=-1.0, bias=1.0)
+        gx = keep.tile([P, LAST], F32, tag="x11", align_bytes=64)
+        nc.scalar.activation(out=gx[:, 0:first], in_=fx_first[:], func=COPY, scale=-1.0, bias=1.0)
+        nc.scalar.activation(out=gx[:, first:LAST], in_=fx_rest[:, 0 : LAST - first], func=COPY, scale=-1.0, bias=1.0)
 
         fy_bank = bank(0)
         nc.tensor.transpose(fy_bank[:, 0:P], fy_rows[:], ident[:])
@@ -149,9 +150,9 @@ def tile_picked_wbilin_none_l_kernel(tc, x_words, x_scales, w1, fx, fy, c00, c01
             for row, (right, left, col) in enumerate((("c01", "c00", gy_col), ("c11", "c10", fy_col))):
                 terms = []
                 if ci == 0:
-                    factors = (fx_first[:], gx_first[:])
+                    factors = (fx_first[:], gx[:, 0:n])
                 else:
-                    factors = (fx_rest[:, v0 - first : v0 - first + n], gx_rest[:, v0 - first : v0 - first + n])
+                    factors = (fx_rest[:, v0 - first : v0 - first + n], gx[:, v0 : v0 + n])
                 for name, factor in zip((right, left), factors):
                     prod = keep.tile([P, n], F32, name="prod_%s_%d" % (name, ci))
                     nc.vector.tensor_tensor(

@@ -16,14 +16,16 @@ U8 = mybir.dt.uint8
 FP8X4 = mybir.dt.float8_e4m3fn_x4
 FP4X4 = mybir.dt.float4_e2m1fn_x4
 MULT = mybir.AluOpType.mult
+ADD = mybir.AluOpType.add
 COPY = mybir.ActivationFunctionType.Copy
 
 P = 128
 PASSES = 2
 BANK = 512
-CHUNKS = (256, 256, 256, 128)
-LAST = T - P
-ADD = mybir.AluOpType.add
+BLOCKS = T // P
+CHUNKS = (512, 256)
+TURNED = sum(CHUNKS)
+DIRECT = T - TURNED
 
 
 def tile_picked_wbilin_none_l_kernel(tc, x_words, x_scales, w1, fx, fy, c00, c01, c10, c11, out):
@@ -35,11 +37,17 @@ def tile_picked_wbilin_none_l_kernel(tc, x_words, x_scales, w1, fx, fy, c00, c01
         def bank(b):
             return psum.tile([P, BANK], F32, name="bank%d" % b, tag="bank%d" % b)
 
+        def blk(b):
+            return slice(P * b, P * (b + 1))
+
         x_planes = keep.tile([P, PASSES * T], U8, align_bytes=64)
         nc.vector.memset(x_planes[:].bitcast(I32), 0)
 
         w_raw = [keep.tile([P, 4, M], F32, name="w_raw%d" % z) for z in range(PASSES)]
-        x_codes = [[keep.tile([P, 2 * BANK], U8, name="x_codes%d_%d" % (z, h), tag="x%d%d" % (z, h), align_bytes=64) for h in range(2)] for z in range(PASSES)]
+        x_codes = [
+            [keep.tile([P, 2 * BANK], U8, name="x_codes%d%d" % (z, h), tag="x_codes%d%d" % (z, h), align_bytes=64) for h in range(2)]
+            for z in range(PASSES)
+        ]
 
         def load_w(z):
             nc.sync.dma_start(out=w_raw[z][:], in_=w1[512 * z : 512 * (z + 1), :].rearrange("(p j) m -> p j m", j=4))
@@ -58,15 +66,19 @@ def tile_picked_wbilin_none_l_kernel(tc, x_words, x_scales, w1, fx, fy, c00, c01
         load_x(0, 1)
         load_x(1, 0)
         load_x(1, 1)
-        first = CHUNKS[0]
-        fx_first = keep.tile([P, first], F32)
-        nc.sync.dma_start(out=fx_first[:], in_=fx[:, 0:first])
+        starts = [sum(CHUNKS[:ci]) for ci in range(len(CHUNKS))]
+        fx_tiles = [keep.tile([P, n], F32, name="fx_tile%d" % ci, tag="fx_tile%d" % ci) for ci, n in enumerate(CHUNKS)]
+        nc.sync.dma_start(out=fx_tiles[0][:], in_=fx[:, 0 : CHUNKS[0]])
         lists = {}
         for name, src in (("c01", c01), ("c00", c00), ("c11", c11), ("c10", c10)):
             lists[name] = keep.tile([P, T // 16], U16, name=name + "_offsets")
             nc.sync.dma_start(lists[name][:], src)
-        fy_rows = keep.tile([P, P], F32)
-        nc.sync.dma_start(out=fy_rows[:], in_=fy[0:16, :].rearrange("r (b i) -> (r b) i", i=P))
+            if name == "c01":
+                f_rows = keep.tile([P, P], F32)
+                for i, f in enumerate((fx, fy)):
+                    nc.sync.dma_start(out=f_rows[64 * i : 64 * (i + 1), :], in_=f[0:8, :].rearrange("r (b i) -> (r b) i", i=P))
+        for ci in range(1, len(CHUNKS)):
+            nc.sync.dma_start(out=fx_tiles[ci][:], in_=fx[:, starts[ci] : starts[ci] + CHUNKS[ci]])
 
         ident = keep.tile([P, P], F32)
         make_identity(nc, ident[:])
@@ -74,21 +86,17 @@ def tile_picked_wbilin_none_l_kernel(tc, x_words, x_scales, w1, fx, fy, c00, c01
         w_codes, w_planes = [], []
         for z in range(PASSES):
             grouped = keep.tile([P, M, 4], BF16, name="w_grouped%d" % z, align_bytes=64)
-            for h in range(2):
-                cols = slice(64 * h, 64 * (h + 1))
-                nc.vector.tensor_copy(out=grouped[:, cols, :], in_=w_raw[z][:, :, cols].rearrange("p j m -> p m j"))
             codes = keep.tile([P, M], U32, name="w_codes%d" % z, align_bytes=64)
             plane = keep.tile([P, M], U8, name="w_plane%d" % z, align_bytes=64)
-            for h in range(2):
-                cols = slice(64 * h, 64 * (h + 1))
+            halves = (slice(0, 64), slice(64, 128))
+            for cols in halves:
+                nc.vector.tensor_copy(out=grouped[:, cols, :], in_=w_raw[z][:, :, cols].rearrange("p j m -> p m j"))
+            for cols in halves:
                 nc.vector.quantize_mx(
                     out=codes[:, cols].bitcast(FP8X4), scales=plane[:, cols], in_=grouped[:, cols, :].rearrange("p m j -> p (m j)")
                 )
             w_codes.append(codes)
             w_planes.append(plane)
-
-        fx_rest = keep.tile([P, T - first], F32)
-        nc.sync.dma_start(out=fx_rest[:], in_=fx[:, first:T])
 
         groups = [(0, 512)] + [(512 + 128 * i, 128) for i in range(4)]
         sums = [bank(g) for g in range(len(groups))]
@@ -110,93 +118,86 @@ def tile_picked_wbilin_none_l_kernel(tc, x_words, x_scales, w1, fx, fy, c00, c01
             else:
                 nc.scalar.copy(out=y[:, c0 : c0 + n], in_=sums[g][:, 0:n])
 
-        gx = keep.tile([P, LAST], F32, tag="x11", align_bytes=64)
-        nc.scalar.activation(out=gx[:, 0:first], in_=fx_first[:], func=COPY, scale=-1.0, bias=1.0)
-        nc.scalar.activation(out=gx[:, first:LAST], in_=fx_rest[:, 0 : LAST - first], func=COPY, scale=-1.0, bias=1.0)
+        gx_tiles = [
+            keep.tile([P, CHUNKS[0]], F32, name="gx_tile0", tag="gx_tile0"),
+            keep.tile([P, CHUNKS[1]], F32, name="gx_tile1", tag="x_codes11", align_bytes=64),
+        ]
+        nc.gpsimd.tensor_scalar(gx_tiles[0][:], fx_tiles[0][:], -1.0, 1.0, MULT, ADD)
+        nc.scalar.activation(out=gx_tiles[1][:], in_=fx_tiles[1][:], func=COPY, scale=-1.0, bias=1.0)
 
-        fy_bank = bank(0)
-        nc.tensor.transpose(fy_bank[:, 0:P], fy_rows[:], ident[:])
-        fy_col = keep.tile([P, 8], F32)
-        gy_col = keep.tile([P, 8], F32)
-        nc.scalar.copy(out=fy_col[:], in_=fy_bank[:, 0:8])
-        nc.scalar.activation(out=gy_col[:], in_=fy_bank[:, 0:8], func=COPY, scale=-1.0, bias=1.0)
+        f_bank = bank(0)
+        nc.tensor.transpose(f_bank[:, 0:P], f_rows[:], ident[:])
+        f_cols = f_bank[:, 0:P].rearrange("p (axis c) -> p axis c", axis=2)[:, :, 0:BLOCKS]
+        sides = keep.tile([P, 2, 2, BLOCKS], F32)
+        nc.scalar.activation(out=sides[:, 0, :, :], in_=f_cols, func=COPY, scale=-1.0, bias=1.0)
+        nc.scalar.copy(out=sides[:, 1, :, :], in_=f_cols)
 
-        def add_transposed(dst, terms):
-            for i, term in enumerate(terms):
-                nc.tensor.matmul(dst, lhsT=term, rhs=ident[:], start=(i == 0), stop=(i == len(terms) - 1), is_transpose=True)
-
-        def blk(b):
-            return slice(P * b, P * (b + 1))
-
-        fx_bank = bank(6)
-        nc.tensor.transpose(fx_bank[:, 0:P], fx_rest[:, LAST - first : T - first], ident[:])
-        gx_col = keep.tile([P, 1], F32)
-        nc.scalar.activation(out=gx_col[:], in_=fx_bank[:, 0:1], func=COPY, scale=-1.0, bias=1.0)
-        corner_col = keep.tile([P, 4], F32)
-        for i, (src, col) in enumerate(((fx_bank, gy_col), (fx_bank, fy_col), (gx_col, gy_col), (gx_col, fy_col))):
-            nc.scalar.activation(out=corner_col[:, i : i + 1], in_=src[:, 0:1], func=COPY, scale=col[:, 7:8])
-        corner_bank = bank(7)
-        for i in range(4):
-            nc.tensor.transpose(corner_bank[:, blk(i)], corner_col[:, i : i + 1].to_broadcast([P, P]), ident[:])
-        corner = keep.tile([P, 4 * P], F32)
-        nc.scalar.copy(out=corner[:], in_=corner_bank[:])
-
-        v0 = 0
-        use = 1
-        tail = keep.tile([P, 2 * P], F32)
-        for ci, n in enumerate(CHUNKS):
-            nb = n // P
-            scaled = []
-            for row, (right, left, col) in enumerate((("c01", "c00", gy_col), ("c11", "c10", fy_col))):
-                terms = []
-                if ci == 0:
-                    factors = (fx_first[:], gx[:, 0:n])
-                else:
-                    factors = (fx_rest[:, v0 - first : v0 - first + n], gx[:, v0 : v0 + n])
-                for name, factor in zip((right, left), factors):
-                    prod = keep.tile([P, n], F32, name="prod_%s_%d" % (name, ci))
-                    nc.vector.tensor_tensor(
-                        prod[:], y[:].indirect(lists[name][:, v0 // 16 : (v0 + n) // 16]), factor, MULT
+        direct_blocks = DIRECT // P
+        corner_cols = keep.tile([P, 2, direct_blocks, 2], F32)
+        corner = keep.tile([P, 2, 2, DIRECT], F32)
+        for row in range(2):
+            for b in range(direct_blocks):
+                vb = TURNED // P + b
+                nc.scalar.activation(out=corner_cols[:, row, b, :], in_=sides[:, :, 0, vb], func=COPY, scale=sides[:, row, 1, vb : vb + 1])
+            spread = bank(5 + row)
+            for side in range(2):
+                for b in range(direct_blocks):
+                    nc.tensor.transpose(
+                        spread[:, blk(side * direct_blocks + b)], corner_cols[:, row, b, side : side + 1].to_broadcast([P, P]), ident[:]
                     )
-                    terms.append(prod)
-                turned = bank(use % 8)
-                use = use + 1
-                for b in range(nb):
-                    add_transposed(turned[:, blk(b)], [t[:, blk(b)] for t in terms])
+            nc.scalar.copy(out=corner[:, row, :, :].rearrange("p s v -> p (s v)"), in_=spread[:, 0 : 2 * DIRECT])
+
+        def add_transposed(dst, term, nb, first):
+            for b in range(nb):
+                nc.tensor.matmul(
+                    dst[:, blk(b)], lhsT=term[:, blk(b)], rhs=ident[:],
+                    start=(first and b == 0), stop=(not first and b == nb - 1), is_transpose=True,
+                )
+
+        def product(prod, name, v0, factor):
+            n = prod.shape[1]
+            nc.vector.tensor_tensor(prod, y[:].indirect(lists[name][:, v0 // 16 : (v0 + n) // 16]), factor, MULT)
+
+        for ci, n in enumerate(CHUNKS):
+            v0 = starts[ci]
+            nb = n // P
+            back = bank(3 + ci % 2)
+            if ci == 0:
+                prods = [keep.tile([P, n], F32, name="prod%d" % i)[:] for i in range(4)]
+            else:
+                lead = keep.tile([P, n], F32, tag="fx_tile0")
+                rest = keep.tile([P, 3 * n], F32, tag="gx_tile0")
+                prods = [lead[:]] + [rest[:, n * i : n * (i + 1)] for i in range(3)]
+            for row, (right, left) in enumerate((("c01", "c00"), ("c11", "c10"))):
+                terms = prods[2 * row : 2 * row + 2]
+                turned = bank(5 * row)
+                product(terms[0], right, v0, fx_tiles[ci][:])
+                add_transposed(turned, terms[0], nb, True)
+                product(terms[1], left, v0, gx_tiles[ci][:])
+                add_transposed(turned, terms[1], nb, False)
                 weighted = keep.tile([P, n], F32, name="weighted_%d_%d" % (row, ci))
                 for b in range(nb):
                     vb = v0 // P + b
-                    nc.scalar.activation(out=weighted[:, blk(b)], in_=turned[:, blk(b)], func=COPY, scale=col[:, vb : vb + 1])
-                scaled.append(weighted)
-            back = bank(use % 8)
-            use = use + 1
-            for b in range(nb):
-                add_transposed(back[:, blk(b)], [t[:, blk(b)] for t in scaled])
-            if ci == len(CHUNKS) - 1:
-                nc.scalar.copy(out=tail[:, 0:P], in_=back[:, 0:n])
-            else:
-                result = keep.tile([P, n], F32, name="result_%d" % ci)
-                nc.scalar.copy(out=result[:], in_=back[:, 0:n])
-                nc.sync.dma_start(out=out[:, v0 : v0 + n], in_=result[:])
-            v0 = v0 + n
+                    nc.scalar.activation(out=weighted[:, blk(b)], in_=turned[:, blk(b)], func=COPY, scale=sides[:, row, 1, vb : vb + 1])
+                add_transposed(back, weighted, nb, row == 0)
+            result = keep.tile([P, n], F32, name="result_%d" % ci)
+            nc.scalar.copy(out=result[:], in_=back[:, 0:n])
+            nc.scalar.dma_start(out=out[:, v0 : v0 + n], in_=result[:])
 
-        def last_product(name, i, a, b):
-            prod = keep.tile([P, b - a], F32, name="last_%s_%d" % (name, a))
-            nc.vector.tensor_tensor(
-                prod[:], y[:].indirect(lists[name][:, (LAST + a) // 16 : (LAST + b) // 16]), corner[:, P * i + a : P * i + b], MULT
-            )
-            return prod
-
-        half = P // 2
-        p01 = last_product("c01", 0, 0, P)
-        p00 = last_product("c00", 2, 0, P)
-        p11 = last_product("c11", 1, 0, P)
-        two = keep.tile([P, P], F32)
-        nc.vector.tensor_tensor(two[:], p01[:], p00[:], ADD)
-        p10a = last_product("c10", 3, 0, half)
-        three = keep.tile([P, P], F32)
-        nc.vector.tensor_tensor(three[:], two[:], p11[:], ADD)
-        p10b = last_product("c10", 3, half, P)
-        nc.vector.tensor_tensor(tail[:, P : P + half], three[:, 0:half], p10a[:], ADD)
-        nc.vector.tensor_tensor(tail[:, P + half : 2 * P], three[:, half:P], p10b[:], ADD)
-        nc.sync.dma_start(out=out[:, LAST - P : T], in_=tail[:])
+        half = DIRECT // 2
+        p01 = keep.tile([P, DIRECT], F32, tag="fx_tile%d" % (len(CHUNKS) - 1))
+        others = keep.tile([P, 3 * DIRECT], F32, tag="x_codes11", align_bytes=64)
+        p00, p11, p10 = [others[:, DIRECT * i : DIRECT * (i + 1)] for i in range(3)]
+        product(p01[:], "c01", TURNED, corner[:, 0, 1, :])
+        product(p00, "c00", TURNED, corner[:, 0, 0, :])
+        product(p11, "c11", TURNED, corner[:, 1, 1, :])
+        two = keep.tile([P, DIRECT], F32)
+        nc.vector.tensor_tensor(two[:], p01[:], p00, ADD)
+        product(p10[:, 0:half], "c10", TURNED, corner[:, 1, 0, 0:half])
+        three = keep.tile([P, DIRECT], F32)
+        nc.vector.tensor_tensor(three[:], two[:], p11, ADD)
+        product(p10[:, half:DIRECT], "c10", TURNED + half, corner[:, 1, 0, half:DIRECT])
+        for h in range(2):
+            four = keep.tile([P, half], F32, name="four%d" % h)
+            nc.vector.tensor_tensor(four[:], three[:, half * h : half * (h + 1)], p10[:, half * h : half * (h + 1)], ADD)
+            nc.sync.dma_start(out=out[:, TURNED + half * h : TURNED + half * (h + 1)], in_=four[:])

from contextlib import ExitStack

import concourse.mybir as mybir
from concourse.masks import make_identity

K, T, M = 1024, 1024, 128
FLOPS = 2 * K * T * M
BYTES = K * T // 2 + K * T // 32 + 4 * K * M + 2 * 4 * T + 4 * 2 * T + 4 * M * T

F32 = mybir.dt.float32
BF16 = mybir.dt.bfloat16
I32 = mybir.dt.int32
U32 = mybir.dt.uint32
U16 = mybir.dt.uint16
U8 = mybir.dt.uint8
FP8X4 = mybir.dt.float8_e4m3fn_x4
FP4X4 = mybir.dt.float4_e2m1fn_x4
MULT = mybir.AluOpType.mult
ADD = mybir.AluOpType.add
COPY = mybir.ActivationFunctionType.Copy

P = 128
PASSES = 2
BANK = 512
BLOCKS = T // P
CHUNKS = (512, 256)
TURNED = sum(CHUNKS)
DIRECT = T - TURNED


def tile_picked_wbilin_none_l_kernel(tc, x_words, x_scales, w1, fx, fy, c00, c01, c10, c11, out):
    nc = tc.nc
    with ExitStack() as ctx:
        keep = ctx.enter_context(tc.tile_pool(name="keep", bufs=1))
        psum = ctx.enter_context(tc.psum_pool(name="psum", bufs=1))

        def bank(b):
            return psum.tile([P, BANK], F32, name="bank%d" % b, tag="bank%d" % b)

        def blk(b):
            return slice(P * b, P * (b + 1))

        x_planes = keep.tile([P, PASSES * T], U8, align_bytes=64)
        nc.vector.memset(x_planes[:].bitcast(I32), 0)

        w_raw = [keep.tile([P, 4, M], F32, name="w_raw%d" % z) for z in range(PASSES)]
        x_codes = [
            [keep.tile([P, 2 * BANK], U8, name="x_codes%d%d" % (z, h), tag="x_codes%d%d" % (z, h), align_bytes=64) for h in range(2)]
            for z in range(PASSES)
        ]

        def load_w(z):
            nc.sync.dma_start(out=w_raw[z][:], in_=w1[512 * z : 512 * (z + 1), :].rearrange("(p j) m -> p j m", j=4))

        def load_x(z, h):
            nc.sync.dma_start(out=x_codes[z][h][:], in_=x_words[z][:, 2 * BANK * h : 2 * BANK * (h + 1)])

        load_w(0)
        load_x(0, 0)
        for r in range(4):
            nc.sync.dma_start(
                out=x_planes[r:P:32, :].bitcast(I32).rearrange("q (z c) -> q z c", z=PASSES),
                in_=x_scales[:, r:16:4, :].bitcast(I32).rearrange("z q c -> q z c"),
            )
        load_w(1)
        load_x(0, 1)
        load_x(1, 0)
        load_x(1, 1)
        starts = [sum(CHUNKS[:ci]) for ci in range(len(CHUNKS))]
        fx_tiles = [keep.tile([P, n], F32, name="fx_tile%d" % ci, tag="fx_tile%d" % ci) for ci, n in enumerate(CHUNKS)]
        nc.sync.dma_start(out=fx_tiles[0][:], in_=fx[:, 0 : CHUNKS[0]])
        lists = {}
        for name, src in (("c01", c01), ("c00", c00), ("c11", c11), ("c10", c10)):
            lists[name] = keep.tile([P, T // 16], U16, name=name + "_offsets")
            nc.sync.dma_start(lists[name][:], src)
            if name == "c01":
                f_rows = keep.tile([P, P], F32)
                for i, f in enumerate((fx, fy)):
                    nc.sync.dma_start(out=f_rows[64 * i : 64 * (i + 1), :], in_=f[0:8, :].rearrange("r (b i) -> (r b) i", i=P))
        for ci in range(1, len(CHUNKS)):
            nc.sync.dma_start(out=fx_tiles[ci][:], in_=fx[:, starts[ci] : starts[ci] + CHUNKS[ci]])

        ident = keep.tile([P, P], F32)
        make_identity(nc, ident[:])

        w_codes, w_planes = [], []
        for z in range(PASSES):
            grouped = keep.tile([P, M, 4], BF16, name="w_grouped%d" % z, align_bytes=64)
            codes = keep.tile([P, M], U32, name="w_codes%d" % z, align_bytes=64)
            plane = keep.tile([P, M], U8, name="w_plane%d" % z, align_bytes=64)
            halves = (slice(0, 64), slice(64, 128))
            for cols in halves:
                nc.vector.tensor_copy(out=grouped[:, cols, :], in_=w_raw[z][:, :, cols].rearrange("p j m -> p m j"))
            for cols in halves:
                nc.vector.quantize_mx(
                    out=codes[:, cols].bitcast(FP8X4), scales=plane[:, cols], in_=grouped[:, cols, :].rearrange("p m j -> p (m j)")
                )
            w_codes.append(codes)
            w_planes.append(plane)

        groups = [(0, 512)] + [(512 + 128 * i, 128) for i in range(4)]
        sums = [bank(g) for g in range(len(groups))]
        y = keep.tile([P, T], F32)
        for z in range(PASSES):
            for g, (c0, n) in enumerate(groups):
                nc.tensor.matmul_mx(
                    out=sums[g][:, 0:n],
                    lhsT=w_codes[z][:].bitcast(FP8X4),
                    lhsT_scale=w_planes[z][:],
                    rhs=x_codes[z][c0 // BANK][:, 2 * (c0 % BANK) : 2 * (c0 % BANK + n)].bitcast(FP4X4),
                    rhs_scale=x_planes[:, z * T + c0 : z * T + c0 + n],
                    start=(z == 0),
                    stop=(z == PASSES - 1),
                )
        for g, (c0, n) in enumerate(groups):
            if g == 0:
                nc.vector.tensor_copy(out=y[:, c0 : c0 + n], in_=sums[g][:, 0:n])
            else:
                nc.scalar.copy(out=y[:, c0 : c0 + n], in_=sums[g][:, 0:n])

        gx_tiles = [
            keep.tile([P, CHUNKS[0]], F32, name="gx_tile0", tag="gx_tile0"),
            keep.tile([P, CHUNKS[1]], F32, name="gx_tile1", tag="x_codes11", align_bytes=64),
        ]
        nc.gpsimd.tensor_scalar(gx_tiles[0][:], fx_tiles[0][:], -1.0, 1.0, MULT, ADD)
        nc.scalar.activation(out=gx_tiles[1][:], in_=fx_tiles[1][:], func=COPY, scale=-1.0, bias=1.0)

        f_bank = bank(0)
        nc.tensor.transpose(f_bank[:, 0:P], f_rows[:], ident[:])
        f_cols = f_bank[:, 0:P].rearrange("p (axis c) -> p axis c", axis=2)[:, :, 0:BLOCKS]
        sides = keep.tile([P, 2, 2, BLOCKS], F32)
        nc.scalar.activation(out=sides[:, 0, :, :], in_=f_cols, func=COPY, scale=-1.0, bias=1.0)
        nc.scalar.copy(out=sides[:, 1, :, :], in_=f_cols)

        direct_blocks = DIRECT // P
        corner_cols = keep.tile([P, 2, direct_blocks, 2], F32)
        corner = keep.tile([P, 2, 2, DIRECT], F32)
        for row in range(2):
            for b in range(direct_blocks):
                vb = TURNED // P + b
                nc.scalar.activation(out=corner_cols[:, row, b, :], in_=sides[:, :, 0, vb], func=COPY, scale=sides[:, row, 1, vb : vb + 1])
            spread = bank(5 + row)
            for side in range(2):
                for b in range(direct_blocks):
                    nc.tensor.transpose(
                        spread[:, blk(side * direct_blocks + b)], corner_cols[:, row, b, side : side + 1].to_broadcast([P, P]), ident[:]
                    )
            nc.scalar.copy(out=corner[:, row, :, :].rearrange("p s v -> p (s v)"), in_=spread[:, 0 : 2 * DIRECT])

        def add_transposed(dst, term, nb, first):
            for b in range(nb):
                nc.tensor.matmul(
                    dst[:, blk(b)], lhsT=term[:, blk(b)], rhs=ident[:],
                    start=(first and b == 0), stop=(not first and b == nb - 1), is_transpose=True,
                )

        def product(prod, name, v0, factor):
            n = prod.shape[1]
            nc.vector.tensor_tensor(prod, y[:].indirect(lists[name][:, v0 // 16 : (v0 + n) // 16]), factor, MULT)

        for ci, n in enumerate(CHUNKS):
            v0 = starts[ci]
            nb = n // P
            back = bank(3 + ci % 2)
            if ci == 0:
                prods = [keep.tile([P, n], F32, name="prod%d" % i)[:] for i in range(4)]
            else:
                lead = keep.tile([P, n], F32, tag="fx_tile0")
                rest = keep.tile([P, 3 * n], F32, tag="gx_tile0")
                prods = [lead[:]] + [rest[:, n * i : n * (i + 1)] for i in range(3)]
            for row, (right, left) in enumerate((("c01", "c00"), ("c11", "c10"))):
                terms = prods[2 * row : 2 * row + 2]
                turned = bank(5 * row)
                product(terms[0], right, v0, fx_tiles[ci][:])
                add_transposed(turned, terms[0], nb, True)
                product(terms[1], left, v0, gx_tiles[ci][:])
                add_transposed(turned, terms[1], nb, False)
                weighted = keep.tile([P, n], F32, name="weighted_%d_%d" % (row, ci))
                for b in range(nb):
                    vb = v0 // P + b
                    nc.scalar.activation(out=weighted[:, blk(b)], in_=turned[:, blk(b)], func=COPY, scale=sides[:, row, 1, vb : vb + 1])
                add_transposed(back, weighted, nb, row == 0)
            result = keep.tile([P, n], F32, name="result_%d" % ci)
            nc.scalar.copy(out=result[:], in_=back[:, 0:n])
            nc.scalar.dma_start(out=out[:, v0 : v0 + n], in_=result[:])

        half = DIRECT // 2
        p01 = keep.tile([P, DIRECT], F32, tag="fx_tile%d" % (len(CHUNKS) - 1))
        others = keep.tile([P, 3 * DIRECT], F32, tag="x_codes11", align_bytes=64)
        p00, p11, p10 = [others[:, DIRECT * i : DIRECT * (i + 1)] for i in range(3)]
        product(p01[:], "c01", TURNED, corner[:, 0, 1, :])
        product(p00, "c00", TURNED, corner[:, 0, 0, :])
        product(p11, "c11", TURNED, corner[:, 1, 1, :])
        two = keep.tile([P, DIRECT], F32)
        nc.vector.tensor_tensor(two[:], p01[:], p00, ADD)
        product(p10[:, 0:half], "c10", TURNED, corner[:, 1, 0, 0:half])
        three = keep.tile([P, DIRECT], F32)
        nc.vector.tensor_tensor(three[:], two[:], p11, ADD)
        product(p10[:, half:DIRECT], "c10", TURNED + half, corner[:, 1, 0, half:DIRECT])
        for h in range(2):
            four = keep.tile([P, half], F32, name="four%d" % h)
            nc.vector.tensor_tensor(four[:], three[:, half * h : half * (h + 1)], p10[:, half * h : half * (h + 1)], ADD)
            nc.sync.dma_start(out=out[:, TURNED + half * h : TURNED + half * (h + 1)], in_=four[:])
